import numpy as np
import ml_dtypes


def mxq(x, axis, fmt="e4m3"):
    dtype, down = {"e4m3": (ml_dtypes.float8_e4m3fn, 7), "e5m2": (ml_dtypes.float8_e5m2, 14)}[fmt]
    v = np.moveaxis(np.asarray(x, np.float32).astype(ml_dtypes.bfloat16).astype(np.float64), axis, -1)
    blocks = v.reshape(v.shape[:-1] + (-1, 32))
    amax = np.abs(blocks).max(-1, keepdims=True)
    byte = np.maximum(np.where(amax > 0, np.frexp(amax)[1] - 1 + 127, 0) - down, 1)
    scale = np.exp2(byte - 127.0)
    codes = (blocks / scale).astype(np.float32).astype(dtype).astype(np.float64)
    return np.moveaxis((codes * scale).reshape(v.shape), -1, axis)


WIDE = False


def mx_kscale(k):
    if not WIDE:
        return np.ones(k)
    levels = np.array([10, -10, 5, -5, 0])
    if k % 512:
        return np.exp2(np.random.permutation(np.resize(levels, k // 32))).repeat(32)
    a = np.empty((k // 512, 16))
    for p in range(k // 512):
        a[p, :8] = np.random.permutation(np.resize(levels, 8))
        for g in range(8):
            far = levels[np.abs(levels - a[p, g]) >= 10]
            a[p, g + 8] = far[np.random.randint(len(far))]
    return np.exp2(a.ravel()).repeat(32)


BF16 = ml_dtypes.bfloat16


def bf(x):
    return np.asarray(x, np.float32).astype(BF16)


def f64(x):
    return np.asarray(x).astype(np.float64)


E2M1 = np.array([0.0, 0.5, 1.0, 1.5, 2.0, 3.0, 4.0, 6.0, -0.0, -0.5, -1.0, -1.5, -2.0, -3.0, -4.0, -6.0])


def pack_weight(w, fmt):
    k, n = w.shape
    w = f64(bf(w)).reshape(k // 32, 32, n)
    amax = np.abs(w).max(1)
    if fmt == "e4m3":
        byte = np.frexp(amax)[1] - 1 + 127 - 7
    else:
        mant, ex = np.frexp(amax / 6.0)
        byte = np.where(mant > 0.5, ex, ex - 1) + 127
    byte = np.clip(np.where(amax > 0, byte, 1), 1, 254)
    scaled = (w * np.exp2(127.0 - byte)[:, None, :]).reshape(k, n).astype(np.float32)
    by_word = np.ascontiguousarray(scaled.reshape(k // 512, 128, 4, n).transpose(0, 1, 3, 2))
    if fmt == "e4m3":
        words = by_word.astype(ml_dtypes.float8_e4m3fn).view(np.uint8)
    else:
        c = by_word.astype(ml_dtypes.float4_e2m1fn).view(np.uint8) & 0xF
        words = c[..., 0::2] | (c[..., 1::2] << 4)
    return np.ascontiguousarray(words), np.ascontiguousarray(byte.astype(np.uint8).reshape(k // 512, 16, n))


def unpack_weight(words, scales, fmt):
    g, p, n, _ = words.shape
    if fmt == "e4m3":
        vals = np.ascontiguousarray(words).view(ml_dtypes.float8_e4m3fn).astype(np.float64)
    else:
        nib = np.empty((g, p, n, 4), np.uint8)
        nib[..., 0::2] = words & 0xF
        nib[..., 1::2] = words >> 4
        vals = E2M1[nib]
    vals = vals * np.repeat(np.exp2(scales.astype(np.float64) - 127.0), 8, axis=1)[..., None]
    return vals.transpose(0, 1, 3, 2).reshape(g * 512, n)

E4M3FN = np.array([(-1.0 if i & 128 else 1.0) * ((1.0 + (i & 7) / 8.0) * 2.0 ** (((i >> 3) & 15) - 7) if i & 120 else (i & 7) * 2.0 ** -9) for i in range(256)])


def e4m3fn_bytes(y):
    return np.clip(np.asarray(y, np.float64), -448.0, 448.0).astype(np.float32).astype(ml_dtypes.float8_e4m3fn).view(np.uint8)


def e4m3fn_values(b):
    return E4M3FN[b]


N, P, Q, M, A = 1024, 512, 1024, 1024, 2


def sigmoid(z):
    return 1.0 / (1.0 + np.exp(-z))


def aipw_score(mu0, mu1, p, t, y):
    return mu1 - mu0 + t * (y - mu1) / p - (1.0 - t) * (y - mu0) / (1.0 - p)


def draw0():
    s, u = mx_kscale(P), mx_kscale(N)
    x = np.random.standard_normal((N, P)) * s
    b = np.random.standard_normal((A, P, Q)) / np.sqrt(P) / s[None, :, None]
    gam = np.random.standard_normal((P, Q)) / np.sqrt(P) / s[:, None]
    gam_words, gam_scales = pack_weight(gam, "e4m3")
    lat = np.random.standard_normal((N, Q))
    y = np.random.standard_normal((N, Q))
    v = np.random.standard_normal((N, M)) / u[:, None]
    w = (1.0 + 0.1 * np.random.standard_normal(N)) * u
    return {"x": bf(x), "b": bf(b), "gam_words": gam_words, "gam_scales": gam_scales, "lat": bf(lat), "y": bf(y), "v": bf(v), "w": bf(w)}


def core(x, b, gam_words, gam_scales, lat, y, v, w):
    xq = mxq(f64(x), 1, "e4m3")
    bb = f64(b)
    mu0 = xq @ mxq(bb[0], 0, "e4m3")
    mu1 = xq @ mxq(bb[1], 0, "e4m3")
    raw = sigmoid(xq @ unpack_weight(gam_words, gam_scales, "e4m3"))
    p = np.minimum(np.maximum(raw, 0.15), 0.85)
    t = np.where(f64(lat) > 0.0, 1.0, 0.0)
    psi = aipw_score(mu0, mu1, p, t, f64(y))
    g = f64(w)[:, None] * psi
    root_n = np.sqrt(x.shape[0])
    return (mxq(f64(v), 0, "e4m3").T @ mxq(g, 0, "e4m3")) / root_n


def setup_inputs():
    drawn = draw0()
    full = np.asarray(drawn['v']).astype(np.float64)
    scale = (np.abs(full).reshape(1024, 8, 128).max(axis=(2,)) / 448.0).astype(np.float32)
    given = {}
    for key, value in drawn.items():
        if key == 'v':
            given['v_bytes'] = e4m3fn_bytes(full / np.repeat(scale.astype(np.float64), 128, axis=1))
            given['v_scale'] = scale
        else:
            given[key] = value
    return given


def reference(x, b, gam_words, gam_scales, lat, y, v_bytes, v_scale, w):
    return core(x, b, gam_words, gam_scales, lat, y, e4m3fn_values(v_bytes) * np.repeat(v_scale.astype(np.float64), 128, axis=1), w)

@@ -1,0 +1,541 @@
+import math
+from contextlib import ExitStack
+
+import concourse.mybir as mybir
+from concourse.masks import make_identity
+
+N, K, Q, M = 1024, 512, 1024, 1024
+FLOPS = 2 * (3 * N * K * Q + N * M * Q)
+
+F32 = mybir.dt.float32
+BF16 = mybir.dt.bfloat16
+I32 = mybir.dt.int32
+U32 = mybir.dt.uint32
+U8 = mybir.dt.uint8
+FP8 = mybir.dt.float8_e4m3fn
+FP8X4 = mybir.dt.float8_e4m3fn_x4
+ALU = mybir.AluOpType
+ACT = mybir.ActivationFunctionType
+
+P = 128
+T = 4
+GROUPS = 2
+HALF = 512
+BANK = 512
+PMIN, PMAX = 0.15, 0.85
+ODDS_LO, ODDS_HI = 3.0 / 17.0, 17.0 / 3.0
+UNITS = (
+    (0, 512, (0,)),
+    (0, 512, (1,)),
+    (512, 256, (0,)),
+    (512, 256, (1,)),
+    (768, 128, (0, 1)),
+    (896, 128, (0, 1)),
+)
+STEP_COLS = 2 * BANK
+
+
+def tile_aipwscorebasismoments_d1p_kernel(
+    tc, x, b, gam_words, gam_scales, lat, y, v_bytes, v_scale, w, out
+):
+    nc = tc.nc
+    x_v = x.rearrange("(g m t) k -> m g t k", g=GROUPS, t=T)
+    b_v = b.rearrange("a (p j) q -> p a j q", j=T)
+    lat_v = lat.rearrange("(g p t) q -> p g t q", g=GROUPS, t=T)
+    y_v = y.rearrange("(g p t) q -> p g t q", g=GROUPS, t=T)
+    v_v = v_bytes.rearrange("(g p t) m -> p g t m", g=GROUPS, t=T)
+    vs_v = v_scale.rearrange("(g p t) j -> p g (t j)", g=GROUPS, t=T)
+    w_v = w.rearrange("(g p t) -> p g t", g=GROUPS, t=T)
+    gam_v = gam_words[0].rearrange("p n t -> p (n t)")
+
+    steps = []
+    for u, (q0, wd, groups) in enumerate(UNITS):
+        slices = [(g, t) for g in groups for t in range(T)]
+        per = STEP_COLS // wd
+        steps += [(u, k, slices[k : k + per]) for k in range(0, len(slices), per)]
+    n_steps = len(steps)
+
+    with ExitStack() as ctx:
+        keep = ctx.enter_context(tc.tile_pool(name="keep", bufs=1))
+        work = ctx.enter_context(tc.tile_pool(name="work", bufs=2))
+        psum = ctx.enter_context(tc.psum_pool(name="psum", bufs=1))
+        ctx.enter_context(tc.manual_schedule())
+
+        ident = keep.tile([P, P], F32, name="ident")
+        xq = keep.tile([P, 2, GROUPS * T, P], U32, name="xq", align_bytes=64)
+        xqs = keep.tile([P, 2, GROUPS * T, P], U8, name="xqs", align_bytes=64)
+        bq = keep.tile([P, 2, Q], U32, name="bq", align_bytes=64)
+        bqs = keep.tile([P, 2, Q], U8, name="bqs", align_bytes=64)
+        gw = keep.tile([P, Q * T], U8, name="gw", align_bytes=64)
+        gs = keep.tile([P, Q], U8, name="gs", align_bytes=64)
+        vq = keep.tile([P, GROUPS, M], U32, name="vq", align_bytes=64)
+        vqs = keep.tile([P, GROUPS, M], U8, name="vqs", align_bytes=64)
+        gq = keep.tile([P, GROUPS, Q], U32, name="gq", align_bytes=64)
+        gqs = keep.tile([P, GROUPS, Q], U8, name="gqs", align_bytes=64)
+        w_sb = keep.tile([P, GROUPS, T], BF16, name="w_sb")
+        wp = keep.tile([P, GROUPS * T], F32, name="wp")
+        vs = keep.tile([P, GROUPS, T * 8], F32, name="vs")
+        zero = keep.tile([P, 1], F32, name="zero")
+        bias = keep.tile([P, 1], F32, name="bias")
+        warm = keep.tile([P, 1], F32, name="warm")
+
+        def load_x(g):
+            xr = work.tile([P, T, K], BF16, name="xr", tag="s4", align_bytes=64)
+            nc.sync.dma_start(out=xr[:], in_=x_v[:, g])
+            return xr
+
+        def load_b(a, h):
+            br = work.tile([P, T, HALF], BF16, name="br", bufs=3)
+            nc.sync.dma_start(out=br[:], in_=b_v[:, a, :, h * HALF : (h + 1) * HALF])
+            return br
+
+        def load_gam(h):
+            cols = slice(h * HALF * T, (h + 1) * HALF * T)
+            nc.sync.dma_start(out=gw[:, cols].bitcast(I32), in_=gam_v[:, cols].bitcast(I32))
+
+        def load_gam_scales():
+            for quad in range(4):
+                nc.sync.dma_start(
+                    out=gs[32 * quad : 32 * quad + 4, :].bitcast(I32),
+                    in_=gam_scales[0, 4 * quad : 4 * quad + 4, :].bitcast(I32),
+                )
+
+        def load_y(h, g):
+            yr = work.tile([P, T, HALF], BF16, name="yr")
+            nc.sync.dma_start(out=yr[:], in_=y_v[:, g, :, h * HALF : (h + 1) * HALF])
+            return yr
+
+        def load_lat(h, g):
+            lr = work.tile([P, T, HALF], BF16, name="lr")
+            nc.sync.dma_start(out=lr[:], in_=lat_v[:, g, :, h * HALF : (h + 1) * HALF])
+            return lr
+
+        def load_v(g):
+            vb = work.tile([P, T, M], U8, name="vb")
+            nc.sync.dma_start(out=vb[:], in_=v_v[:, g])
+            return vb
+
+        xg = {}
+        xps = {}
+        xn = {}
+
+        def x_transpose(g, tags):
+            words = xr[g][:].bitcast(F32)
+            xps[g] = []
+            for half in range(2):
+                xp = psum.tile([P, 2, 2, P], F32, name="xp", tag=tags[half])
+                for i in range(2):
+                    for u in range(2):
+                        nc.tensor.transpose(xp[:, i, u, :], words[:, 2 * half + i, u : K // 2 : 2], ident[:])
+                xps[g].append(xp)
+            xg[g] = work.tile([P, T, P, T], BF16, name="xg", tag="s4b", bufs=3, align_bytes=64)
+
+        def x_copy(g, half, copy):
+            copy(
+                out=xg[g][:, 2 * half : 2 * half + 2].bitcast(F32),
+                in_=xps[g][half][:].rearrange("p s u r -> p s r u"),
+            )
+
+        def quantize_x(g, sign):
+            words = slice(g * T, (g + 1) * T)
+            src = xg[g][:].rearrange("p s r t -> p (s r t)") if sign == 0 else xn[g][:]
+            nc.vector.quantize_mx(
+                out=xq[:, sign, words, :].rearrange("p s r -> p (s r)").bitcast(FP8X4),
+                scales=xqs[:, sign, words, :].rearrange("p s r -> p (s r)"),
+                in_=src,
+            )
+
+        def negate_x(g):
+            xn[g] = work.tile([P, T * P * T], BF16, name="xn", bufs=1, align_bytes=64)
+            nc.vector.tensor_scalar(
+                out=xn[g][:], in0=xg[g][:].rearrange("p s r t -> p (s r t)"), scalar1=-1.0, scalar2=None, op0=ALU.mult
+            )
+
+        def interleave(copy, dst, src):
+            copy(
+                out=dst.rearrange("p (c i) t -> p c t i", i=4),
+                in_=src.rearrange("p t (c i) -> p c t i", i=4),
+            )
+
+        bi = {}
+
+        def b_interleave(a, h, copy, lo, hi):
+            if (a, h) not in bi:
+                bi[a, h] = work.tile([P, HALF, T], BF16, name="bi", align_bytes=64)
+            interleave(copy, bi[a, h][:, lo:hi, :], br[a, h][:, :, lo:hi])
+
+        def quantize_b(a, h):
+            cols = slice(h * HALF, (h + 1) * HALF)
+            nc.vector.quantize_mx(
+                out=bq[:, a, cols].bitcast(FP8X4), scales=bqs[:, a, cols], in_=bi[a, h][:].rearrange("p q t -> p (q t)")
+            )
+
+        vw = {}
+        vi = {}
+
+        def v_widen(g, t):
+            if t == 0:
+                vw[g] = work.tile([P, T, M], BF16, name="vw", bufs=1)
+            for j in range(8):
+                cols = slice(j * P, (j + 1) * P)
+                nc.scalar.activation(
+                    out=vw[g][:, t, cols],
+                    in_=vb[g][:, t, cols].bitcast(FP8),
+                    func=ACT.Copy,
+                    scale=vs[:, g, t * 8 + j : t * 8 + j + 1],
+                )
+
+        def v_interleave(g, copy, lo, hi):
+            if g not in vi:
+                vi[g] = work.tile([P, M, T], BF16, name="vi", bufs=1, align_bytes=64)
+            interleave(copy, vi[g][:, lo:hi, :], vw[g][:, :, lo:hi])
+
+        def quantize_v(g):
+            nc.vector.quantize_mx(
+                out=vq[:, g, :].bitcast(FP8X4), scales=vqs[:, g, :], in_=vi[g][:].rearrange("p m t -> p (m t)")
+            )
+
+        yw = {}
+        tb = {}
+
+        def weigh_y(h, g, engines):
+            yw[h, g] = work.tile([P, T, HALF], F32, name="yw")
+            for t in range(T):
+                dst, src, by = yw[h, g][:, t, :], yr[h, g][:, t, :], wp[:, g * T + t : g * T + t + 1]
+                if engines[t] == "s":
+                    nc.scalar.activation(out=dst, in_=src, func=ACT.Copy, scale=by)
+                else:
+                    engine = nc.vector if engines[t] == "v" else nc.gpsimd
+                    engine.tensor_scalar(out=dst, in0=src, scalar1=by, scalar2=1.0, op0=ALU.mult, op1=ALU.mult)
+
+        def treat(h, g):
+            tb[h, g] = work.tile([P, T, HALF], F32, name="tb")
+            nc.vector.tensor_scalar(
+                out=tb[h, g][:], in0=lr[h, g][:], scalar1=0.0, scalar2=PMIN, op0=ALU.is_gt, op1=ALU.subtract
+            )
+
+        def mx(o, lhs, rhs, start, stop):
+            nc.tensor.matmul_mx(
+                out=o, lhsT=lhs[0], lhsT_scale=lhs[1], rhs=rhs[0], rhs_scale=rhs[1], start=start, stop=stop
+            )
+
+        def x_op(sign, g, t):
+            return xq[:, sign, g * T + t, :].bitcast(FP8X4), xqs[:, sign, g * T + t, :]
+
+        def b_op(a, q0, wd):
+            return bq[:, a, q0 : q0 + wd].bitcast(FP8X4), bqs[:, a, q0 : q0 + wd]
+
+        def gam_op(q0, wd):
+            return gw[:, q0 * T : (q0 + wd) * T].bitcast(FP8X4), gs[:, q0 : q0 + wd]
+
+        banks = {}
+
+        def places(n):
+            u, k0, slices = steps[n]
+            wd = UNITS[u][1]
+            return [(g, t, i * wd // BANK, i * wd % BANK) for i, (g, t) in enumerate(slices)]
+
+        def new_banks(kind, n):
+            banks[kind, n] = [psum.tile([P, BANK], F32, name=kind, tag="%s%d" % (kind, j)) for j in range(2)]
+            return banks[kind, n]
+
+        def pe_z(n):
+            q0, wd = UNITS[steps[n][0]][:2]
+            o = new_banks("z", n)
+            for g, t, j, col in places(n):
+                mx(o[j][:, col : col + wd], x_op(0, g, t), gam_op(q0, wd), True, True)
+
+        def pe_mu0(n):
+            q0, wd = UNITS[steps[n][0]][:2]
+            o = new_banks("m", n)
+            for g, t, j, col in places(n):
+                mx(o[j][:, col : col + wd], x_op(0, g, t), b_op(0, q0, wd), True, True)
+
+        def pe_d(n):
+            q0, wd = UNITS[steps[n][0]][:2]
+            o = new_banks("d", n)
+            for g, t, j, col in places(n):
+                mx(o[j][:, col : col + wd], x_op(0, g, t), b_op(1, q0, wd), True, False)
+                mx(o[j][:, col : col + wd], x_op(1, g, t), b_op(0, q0, wd), False, True)
+
+        raw = {}
+        odds = {}
+        kap = {}
+        res = {}
+        dd = {}
+        gi = {}
+
+        def unit_tile(store, u, name, bufs):
+            q0, wd, groups = UNITS[u]
+            if u not in store:
+                size = len(groups) * T * wd
+                tag, n_bufs = bufs[size]
+                store[u] = work.tile([P, size], F32, name=name, tag=tag, bufs=n_bufs, align_bytes=64)
+            return store[u]
+
+        def s_exp(n):
+            u, k0, slices = steps[n]
+            base = k0 * UNITS[u][1]
+            k = unit_tile(kap, u, "kap", {2048: ("kap", 2), 1024: ("s4b", 3)})
+            raw[n] = work.tile([P, STEP_COLS], F32, name="raw")
+            for j in range(2):
+                nc.scalar.activation(
+                    out=k[:, base + j * BANK : base + (j + 1) * BANK],
+                    in_=banks["z", n][j][:],
+                    func=ACT.Exp,
+                    scale=-1.0,
+                    bias=bias[:],
+                )
+                nc.scalar.activation(out=raw[n][:, j * BANK : (j + 1) * BANK], in_=banks["z", n][j][:], func=ACT.Exp)
+
+        def clip(n, engine=nc.gpsimd):
+            odds[n] = work.tile([P, STEP_COLS], F32, name="odds", bufs=1)
+            engine.tensor_scalar(
+                out=odds[n][:], in0=raw[n][:], scalar1=ODDS_HI, scalar2=ODDS_LO, op0=ALU.min, op1=ALU.max
+            )
+
+        def v_h(n):
+            q0, wd = UNITS[steps[n][0]][:2]
+            off = q0 % HALF
+            res[n] = work.tile([P, STEP_COLS], F32, name="res")
+            for g, t, j, col in places(n):
+                nc.vector.scalar_tensor_tensor(
+                    out=res[n][:, j * BANK + col : j * BANK + col + wd],
+                    in0=banks["m", n][j][:, col : col + wd],
+                    scalar=wp[:, g * T + t : g * T + t + 1],
+                    in1=yw[q0 // HALF, g][:, t, off : off + wd],
+                    op0=ALU.mult,
+                    op1=ALU.subtract,
+                )
+
+        def v_kap(n):
+            u, k0, slices = steps[n]
+            q0, wd, groups = UNITS[u]
+            off = q0 % HALF
+            for i in range(0, len(slices), T):
+                part = slices[i : i + T]
+                g, t0 = part[0]
+                lo, hi = (k0 + i) * wd, (k0 + i + len(part)) * wd
+                k3 = kap[u][:, lo:hi].rearrange("p (t q) -> p t q", q=wd)
+                nc.vector.scalar_tensor_tensor(
+                    out=k3,
+                    in0=k3,
+                    scalar=PMIN * ODDS_LO,
+                    in1=tb[q0 // HALF, g][:, t0 : t0 + len(part), off : off + wd],
+                    op0=ALU.max,
+                    op1=ALU.min,
+                )
+
+        def v_f(n):
+            nc.vector.scalar_tensor_tensor(
+                out=res[n][:], in0=odds[n][:], scalar=1.0, in1=res[n][:], op0=ALU.add, op1=ALU.mult
+            )
+
+        def v_d(n):
+            u, k0, slices = steps[n]
+            q0, wd = UNITS[u][:2]
+            d = unit_tile(dd, u, "dd", {2048: ("dd", 2), 1024: ("dd", 2)})
+            for i, (g, t, j, col) in enumerate(places(n)):
+                lo = (k0 + i) * wd
+                nc.vector.scalar_tensor_tensor(
+                    out=d[:, lo : lo + wd],
+                    in0=banks["d", n][j][:, col : col + wd],
+                    scalar=wp[:, g * T + t : g * T + t + 1],
+                    in1=res[n][:, j * BANK + col : j * BANK + col + wd],
+                    op0=ALU.mult,
+                    op1=ALU.add,
+                )
+
+        def v_g(u, i, lo, hi):
+            q0, wd, groups = UNITS[u]
+            if u not in gi:
+                gi[u] = work.tile([P, len(groups), wd, T], BF16, name="gi", tag="s4", align_bytes=64)
+            side = slice(i * T * wd, (i + 1) * T * wd)
+            k3 = kap[u][:, side].rearrange("p (t q) -> p t q", t=T)[:, :, lo:hi]
+            d3 = dd[u][:, side].rearrange("p (t q) -> p t q", t=T)[:, :, lo:hi]
+            nc.vector.tensor_tensor(
+                out=gi[u][:, i, lo:hi, :].rearrange("p (c i) t -> p c t i", i=4),
+                in0=k3.rearrange("p t (c i) -> p c t i", i=4),
+                in1=d3.rearrange("p t (c i) -> p c t i", i=4),
+                op=ALU.mult,
+            )
+
+        def quantize_g(u, i):
+            q0, wd, groups = UNITS[u]
+            nc.vector.quantize_mx(
+                out=gq[:, groups[i], q0 : q0 + wd].bitcast(FP8X4),
+                scales=gqs[:, groups[i], q0 : q0 + wd],
+                in_=gi[u][:, i].rearrange("p q t -> p (q t)"),
+            )
+
+        def v_op(g, m):
+            return vq[:, g, m * P : (m + 1) * P].bitcast(FP8X4), vqs[:, g, m * P : (m + 1) * P]
+
+        def gq_op(g, q0, wd):
+            return gq[:, g, q0 : q0 + wd].bitcast(FP8X4), gqs[:, g, q0 : q0 + wd]
+
+        def moments(q0, wd, job, tag, engine="s"):
+            per = BANK // wd
+            o = psum.tile([P, BANK], F32, name="o", tag=tag)
+            for i in range(per):
+                m = job * per + i
+                for g in range(GROUPS):
+                    mx(o[:, i * wd : (i + 1) * wd], v_op(g, m), gq_op(g, q0, wd), g == 0, g == 1)
+            ot = work.tile([P, BANK], F32, name="ot", bufs=6)
+            if engine == "s":
+                nc.scalar.activation(out=ot[:], in_=o[:], func=ACT.Copy, scale=1.0 / 32.0)
+            else:
+                nc.vector.tensor_scalar(out=ot[:], in0=o[:], scalar1=1.0 / 32.0, scalar2=None, op0=ALU.mult)
+            rows = slice(job * per * P, (job + 1) * per * P)
+            nc.sync.dma_start(
+                out=out[rows, q0 : q0 + wd].rearrange("(i m) q -> m i q", i=per),
+                in_=ot[:].rearrange("m (i q) -> m i q", i=per),
+            )
+
+        S, V = nc.scalar.copy, nc.vector.tensor_copy
+
+        nc.vector.memset(gs[:].bitcast(I32), 0)
+        nc.vector.memset(zero[:], 0.0)
+        nc.vector.tensor_scalar(out=bias[:], in0=zero[:], scalar1=math.log(PMIN), scalar2=None, op0=ALU.add)
+        nc.scalar.activation(out=warm[:], in_=zero[:], func=ACT.Exp)
+        make_identity(nc, ident[:])
+
+        xr, br, yr, lr, vb = {}, {}, {}, {}, {}
+        xr[0] = load_x(0)
+        load_gam_scales()
+        nc.sync.dma_start(out=w_sb[:], in_=w_v)
+        br[0, 0] = load_b(0, 0)
+        yr[0, 0] = load_y(0, 0)
+        load_gam(0)
+        lr[0, 0] = load_lat(0, 0)
+        br[1, 0] = load_b(1, 0)
+        xr[1] = load_x(1)
+        yr[0, 1] = load_y(0, 1)
+        br[0, 1] = load_b(0, 1)
+        nc.sync.dma_start(out=vs[:], in_=vs_v)
+        vb[0] = load_v(0)
+        lr[0, 1] = load_lat(0, 1)
+        vb[1] = load_v(1)
+        nc.vector.tensor_scalar(
+            out=wp[:],
+            in0=w_sb[:].rearrange("p g t -> p (g t)"),
+            scalar1=-1.0 / PMIN,
+            scalar2=None,
+            op0=ALU.mult,
+        )
+
+        x_transpose(0, ("o0", "o1"))
+        x_copy(0, 0, S)
+        x_copy(0, 1, V)
+        quantize_x(0, 0)
+        weigh_y(0, 0, "vvgg")
+        b_interleave(0, 0, V, 0, 256)
+        b_interleave(0, 0, S, 256, 512)
+        negate_x(0)
+        quantize_b(0, 0)
+        pe_z(0)
+        pe_mu0(0)
+        s_exp(0)
+        quantize_x(0, 1)
+
+        def step(n, early=(), mid=(), pe=(), fill=()):
+            v_h(n)
+            if n > 0:
+                v_d(n - 1)
+                pe_d(n)
+            for f in early:
+                f()
+            v_kap(n)
+            for f in mid:
+                f()
+            for f in pe:
+                f()
+            if n + 1 < n_steps:
+                pe_z(n + 1)
+                pe_mu0(n + 1)
+                s_exp(n + 1)
+            v_f(n)
+            if n + 1 < n_steps:
+                clip(n + 1)
+            for f in fill:
+                f()
+
+        v_h(0)
+        clip(0, nc.vector)
+        b_interleave(1, 0, V, 0, 256)
+        b_interleave(1, 0, S, 256, 512)
+        treat(0, 0)
+        quantize_b(1, 0)
+        v_kap(0)
+        pe_z(1)
+        pe_mu0(1)
+        s_exp(1)
+        v_f(0)
+        clip(1)
+        weigh_y(0, 1, "gggg")
+        x_transpose(1, ("o0", "o1"))
+        pe_d(0)
+        x_copy(1, 0, S)
+        x_copy(1, 1, S)
+        b_interleave(0, 1, S, 0, 512)
+        v_widen(0, 0)
+
+        br[1, 1] = load_b(1, 1)
+        load_gam(1)
+        yr[1, 0] = load_y(1, 0)
+        lr[1, 0] = load_lat(1, 0)
+        yr[1, 1] = load_y(1, 1)
+
+        def late_lat():
+            lr[1, 1] = load_lat(1, 1)
+
+        step(
+            1,
+            mid=[lambda: quantize_x(1, 0), lambda: negate_x(1), lambda: treat(0, 1), lambda: quantize_x(1, 1)],
+            fill=[lambda: b_interleave(1, 1, S, 0, 512), lambda: weigh_y(1, 0, "ssss"), late_lat, lambda: v_widen(0, 1)],
+        )
+        step(
+            2,
+            mid=[lambda: v_g(0, 0, 0, 256), lambda: quantize_b(0, 1)],
+            fill=[lambda: v_widen(0, 2), lambda: v_widen(0, 3), lambda: v_interleave(0, S, 0, 512)],
+        )
+        step(
+            3,
+            mid=[lambda: v_g(0, 0, 256, 512), lambda: quantize_b(1, 1), lambda: treat(1, 0), lambda: quantize_g(0, 0)],
+            fill=[lambda: weigh_y(1, 1, "ssss"), lambda: v_interleave(0, S, 512, 1024)],
+        )
+        step(
+            4,
+            mid=[lambda: v_g(1, 0, 0, 256), lambda: v_g(1, 0, 256, 512)],
+            fill=[lambda t=t: v_widen(1, t) for t in range(4)],
+        )
+        step(
+            5,
+            early=[lambda: treat(1, 1)],
+            mid=[lambda: quantize_g(1, 0), lambda: v_g(2, 0, 0, 256), lambda: quantize_v(0)],
+            fill=[lambda: v_interleave(1, S, 0, 512), lambda: v_interleave(1, S, 512, 1024)],
+        )
+        step(
+            6,
+            mid=[lambda: quantize_g(2, 0), lambda: v_g(3, 0, 0, 256)],
+            pe=[lambda: quantize_v(1)],
+            fill=[lambda j=j: moments(0, 512, j, "o%d" % (j % 2)) for j in range(4)],
+        )
+        step(
+            7,
+            mid=[lambda: quantize_g(3, 0), lambda: v_g(4, 0, 0, 128), lambda: v_g(4, 1, 0, 128)],
+            fill=[lambda j=j: moments(0, 512, j, "o%d" % (j % 2)) for j in range(4, 8)],
+        )
+        quantize_g(4, 0)
+        quantize_g(4, 1)
+        v_d(7)
+        for j in range(4):
+            moments(512, 256, j, "zm"[j // 2] + str(j % 2))
+        v_g(5, 0, 0, 128)
+        v_g(5, 1, 0, 128)
+        for j in range(2):
+            moments(768, 128, j, "o%d" % j)
+        quantize_g(5, 0)
+        quantize_g(5, 1)
+        moments(896, 128, 0, "d0", "s")
+        moments(896, 128, 1, "d1", "v")

@@ -145,13 +145,18 @@ def tile_aipwscorebasismoments_d1p_kernel(
                 in_=src,
             )
 
-        def negate_x(g):
+        def negate_x(g, engine):
             xn[g] = work.tile([P, T * P * T], BF16, name="xn", bufs=1, align_bytes=64)
-            nc.vector.tensor_scalar(
-                out=xn[g][:], in0=xg[g][:].rearrange("p s r t -> p (s r t)"), scalar1=-1.0, scalar2=None, op0=ALU.mult
-            )
+            src = xg[g][:].rearrange("p s r t -> p (s r t)")
+            if engine == "s":
+                nc.scalar.activation(out=xn[g][:], in_=src, func=ACT.Copy, scale=-1.0)
+            else:
+                nc.vector.tensor_scalar(out=xn[g][:], in0=src, scalar1=-1.0, scalar2=None, op0=ALU.mult)
 
         def interleave(copy, dst, src):
+            if copy is G:
+                copy(out=dst, in_=src.rearrange("p t q -> p q t"))
+                return
             copy(
                 out=dst.rearrange("p (c i) t -> p c t i", i=4),
                 in_=src.rearrange("p t (c i) -> p c t i", i=4),
@@ -199,8 +204,11 @@ def tile_aipwscorebasismoments_d1p_kernel(
         tb = {}
 
         def weigh_y(h, g, engines):
-            yw[h, g] = work.tile([P, T, HALF], F32, name="yw")
+            if (h, g) not in yw:
+                yw[h, g] = work.tile([P, T, HALF], F32, name="yw")
             for t in range(T):
+                if engines[t] == "-":
+                    continue
                 dst, src, by = yw[h, g][:, t, :], yr[h, g][:, t, :], wp[:, g * T + t : g * T + t + 1]
                 if engines[t] == "s":
                     nc.scalar.activation(out=dst, in_=src, func=ACT.Copy, scale=by)
@@ -331,11 +339,11 @@ def tile_aipwscorebasismoments_d1p_kernel(
                 out=res[n][:], in0=odds[n][:], scalar=1.0, in1=res[n][:], op0=ALU.add, op1=ALU.mult
             )
 
-        def v_d(n):
+        def v_d(n, part=slice(None)):
             u, k0, slices = steps[n]
             q0, wd = UNITS[u][:2]
             d = unit_tile(dd, u, "dd", {2048: ("dd", 2), 1024: ("dd", 2)})
-            for i, (g, t, j, col) in enumerate(places(n)):
+            for i, (g, t, j, col) in list(enumerate(places(n)))[part]:
                 lo = (k0 + i) * wd
                 nc.vector.scalar_tensor_tensor(
                     out=d[:, lo : lo + wd],
@@ -374,25 +382,32 @@ def tile_aipwscorebasismoments_d1p_kernel(
         def gq_op(g, q0, wd):
             return gq[:, g, q0 : q0 + wd].bitcast(FP8X4), gqs[:, g, q0 : q0 + wd]
 
-        def moments(q0, wd, job, tag, engine="s"):
+        def scale_out(engine, dst, src):
+            if engine == "s":
+                nc.scalar.activation(out=dst, in_=src, func=ACT.Copy, scale=1.0 / 32.0)
+            else:
+                nc.vector.tensor_scalar(out=dst, in0=src, scalar1=1.0 / 32.0, scalar2=None, op0=ALU.mult)
+
+        def store(ot, q0, wd, m0, tiles):
+            nc.sync.dma_start(
+                out=out[m0 * P : (m0 + tiles) * P, q0 : q0 + wd].rearrange("(i m) q -> m i q", i=tiles),
+                in_=ot[:, 0 : tiles * wd].rearrange("m (i q) -> m i q", i=tiles),
+            )
+
+        def moments(q0, wd, job, tag, engine):
             per = BANK // wd
             o = psum.tile([P, BANK], F32, name="o", tag=tag)
             for i in range(per):
-                m = job * per + i
                 for g in range(GROUPS):
-                    mx(o[:, i * wd : (i + 1) * wd], v_op(g, m), gq_op(g, q0, wd), g == 0, g == 1)
-            ot = work.tile([P, BANK], F32, name="ot", bufs=6)
-            if engine == "s":
-                nc.scalar.activation(out=ot[:], in_=o[:], func=ACT.Copy, scale=1.0 / 32.0)
-            else:
-                nc.vector.tensor_scalar(out=ot[:], in0=o[:], scalar1=1.0 / 32.0, scalar2=None, op0=ALU.mult)
-            rows = slice(job * per * P, (job + 1) * per * P)
-            nc.sync.dma_start(
-                out=out[rows, q0 : q0 + wd].rearrange("(i m) q -> m i q", i=per),
-                in_=ot[:].rearrange("m (i q) -> m i q", i=per),
-            )
+                    mx(o[:, i * wd : (i + 1) * wd], v_op(g, job * per + i), gq_op(g, q0, wd), g == 0, g == 1)
+            ot = work.tile([P, BANK], F32, name="ot", bufs=9)
+            scale_out(engine, ot[:], o[:])
+            store(ot, q0, wd, job * per, per)
 
         S, V = nc.scalar.copy, nc.vector.tensor_copy
+
+        def G(out, in_):
+            nc.gpsimd.tensor_scalar(out=out, in0=in_, scalar1=1.0, scalar2=0.0, op0=ALU.mult, op1=ALU.add)
 
         nc.vector.memset(gs[:].bitcast(I32), 0)
         nc.vector.memset(zero[:], 0.0)
@@ -402,20 +417,17 @@ def tile_aipwscorebasismoments_d1p_kernel(
 
         xr, br, yr, lr, vb = {}, {}, {}, {}, {}
         xr[0] = load_x(0)
-        load_gam_scales()
         nc.sync.dma_start(out=w_sb[:], in_=w_v)
         br[0, 0] = load_b(0, 0)
         yr[0, 0] = load_y(0, 0)
+        load_gam_scales()
         load_gam(0)
-        lr[0, 0] = load_lat(0, 0)
         br[1, 0] = load_b(1, 0)
-        xr[1] = load_x(1)
-        yr[0, 1] = load_y(0, 1)
-        br[0, 1] = load_b(0, 1)
+        lr[0, 0] = load_lat(0, 0)
         nc.sync.dma_start(out=vs[:], in_=vs_v)
-        vb[0] = load_v(0)
-        lr[0, 1] = load_lat(0, 1)
-        vb[1] = load_v(1)
+        xr[1] = load_x(1)
+        br[0, 1] = load_b(0, 1)
+        yr[0, 1] = load_y(0, 1)
         nc.vector.tensor_scalar(
             out=wp[:],
             in0=w_sb[:].rearrange("p g t -> p (g t)"),
@@ -428,114 +440,131 @@ def tile_aipwscorebasismoments_d1p_kernel(
         x_copy(0, 0, S)
         x_copy(0, 1, V)
         quantize_x(0, 0)
-        weigh_y(0, 0, "vvgg")
+        weigh_y(0, 0, "vv--")
         b_interleave(0, 0, V, 0, 256)
         b_interleave(0, 0, S, 256, 512)
-        negate_x(0)
+        negate_x(0, "v")
         quantize_b(0, 0)
+        quantize_x(0, 1)
         pe_z(0)
         pe_mu0(0)
+        b_interleave(1, 0, G, 0, 256)
         s_exp(0)
-        quantize_x(0, 1)
-
-        def step(n, early=(), mid=(), pe=(), fill=()):
-            v_h(n)
-            if n > 0:
-                v_d(n - 1)
-                pe_d(n)
-            for f in early:
-                f()
-            v_kap(n)
-            for f in mid:
-                f()
-            for f in pe:
-                f()
-            if n + 1 < n_steps:
-                pe_z(n + 1)
-                pe_mu0(n + 1)
-                s_exp(n + 1)
-            v_f(n)
-            if n + 1 < n_steps:
-                clip(n + 1)
-            for f in fill:
-                f()
-
-        v_h(0)
-        clip(0, nc.vector)
-        b_interleave(1, 0, V, 0, 256)
         b_interleave(1, 0, S, 256, 512)
-        treat(0, 0)
-        quantize_b(1, 0)
-        v_kap(0)
+        weigh_y(0, 0, "--ss")
         pe_z(1)
-        pe_mu0(1)
         s_exp(1)
+        v_h(0)
+        treat(0, 0)
+        clip(0, nc.vector)
+        quantize_b(1, 0)
+        pe_mu0(1)
         v_f(0)
         clip(1)
-        weigh_y(0, 1, "gggg")
+        v_kap(0)
         x_transpose(1, ("o0", "o1"))
         pe_d(0)
         x_copy(1, 0, S)
         x_copy(1, 1, S)
-        b_interleave(0, 1, S, 0, 512)
-        v_widen(0, 0)
-
+        weigh_y(0, 1, "ssss")
         br[1, 1] = load_b(1, 1)
         load_gam(1)
+        lr[0, 1] = load_lat(0, 1)
         yr[1, 0] = load_y(1, 0)
+        vb[0] = load_v(0)
         lr[1, 0] = load_lat(1, 0)
-        yr[1, 1] = load_y(1, 1)
+        vb[1] = load_v(1)
 
-        def late_lat():
+        def step(n, late_z=False, then=(), end=(), scalar=()):
+            if n + 1 < n_steps and not late_z:
+                pe_z(n + 1)
+                s_exp(n + 1)
+            v_d(n - 1)
+            v_h(n)
+            pe_d(n)
+            if n + 1 < n_steps and not late_z:
+                pe_mu0(n + 1)
+            for f in then:
+                f()
+            if late_z:
+                pe_z(n + 1)
+                s_exp(n + 1)
+                pe_mu0(n + 1)
+            v_f(n)
+            if n + 1 < n_steps:
+                clip(n + 1)
+            for f in end:
+                f()
+            v_kap(n)
+            for f in scalar:
+                f()
+
+        def late_loads():
+            yr[1, 1] = load_y(1, 1)
             lr[1, 1] = load_lat(1, 1)
 
+        def out_jobs(lo, hi, engine="s"):
+            banks_free = ("o0", "o1", "z0", "z1", "m0", "m1")
+            jobs = [(0, 512, j) for j in range(8)] + [(512, 256, j) for j in range(4)] + [(768, 128, j) for j in range(2)]
+            for i in range(lo, hi):
+                moments(*jobs[i], banks_free[i % 6], engine)
+
+        b_interleave(0, 1, S, 0, 512)
         step(
             1,
-            mid=[lambda: quantize_x(1, 0), lambda: negate_x(1), lambda: treat(0, 1), lambda: quantize_x(1, 1)],
-            fill=[lambda: b_interleave(1, 1, S, 0, 512), lambda: weigh_y(1, 0, "ssss"), late_lat, lambda: v_widen(0, 1)],
+            late_z=True,
+            then=[lambda: quantize_x(1, 0), lambda: negate_x(1, "v"), lambda: treat(0, 1)],
+            end=[lambda: quantize_x(1, 1)],
+            scalar=[lambda: b_interleave(1, 1, G, 0, 128), lambda: b_interleave(1, 1, S, 128, 512), late_loads],
         )
         step(
             2,
-            mid=[lambda: v_g(0, 0, 0, 256), lambda: quantize_b(0, 1)],
-            fill=[lambda: v_widen(0, 2), lambda: v_widen(0, 3), lambda: v_interleave(0, S, 0, 512)],
+            then=[lambda: v_g(0, 0, 0, 256), lambda: v_g(0, 0, 256, 512)],
+            end=[lambda: quantize_b(0, 1)],
+            scalar=[lambda: weigh_y(1, 0, "ssss")] + [lambda t=t: v_widen(0, t) for t in range(4)],
         )
         step(
             3,
-            mid=[lambda: v_g(0, 0, 256, 512), lambda: quantize_b(1, 1), lambda: treat(1, 0), lambda: quantize_g(0, 0)],
-            fill=[lambda: weigh_y(1, 1, "ssss"), lambda: v_interleave(0, S, 512, 1024)],
+            then=[lambda: quantize_b(1, 1), lambda: quantize_g(0, 0)],
+            scalar=[lambda: treat(1, 0), lambda: weigh_y(1, 1, "ssss"), lambda: v_interleave(0, G, 0, 128), lambda: v_interleave(0, S, 128, 512)],
         )
         step(
             4,
-            mid=[lambda: v_g(1, 0, 0, 256), lambda: v_g(1, 0, 256, 512)],
-            fill=[lambda t=t: v_widen(1, t) for t in range(4)],
+            then=[lambda: v_g(1, 0, 0, 256), lambda: v_g(1, 0, 256, 512)],
+            scalar=[lambda: v_interleave(0, G, 512, 640), lambda: v_interleave(0, S, 640, 1024)] + [lambda t=t: v_widen(1, t) for t in range(3)],
         )
         step(
             5,
-            early=[lambda: treat(1, 1)],
-            mid=[lambda: quantize_g(1, 0), lambda: v_g(2, 0, 0, 256), lambda: quantize_v(0)],
-            fill=[lambda: v_interleave(1, S, 0, 512), lambda: v_interleave(1, S, 512, 1024)],
+            then=[lambda: quantize_g(1, 0), lambda: v_g(2, 0, 0, 256), lambda: quantize_v(0), lambda: treat(1, 1)],
+            scalar=[lambda: v_widen(1, 3), lambda: v_interleave(1, G, 0, 128), lambda: v_interleave(1, S, 128, 512), lambda: v_interleave(1, S, 512, 1024)],
         )
         step(
             6,
-            mid=[lambda: quantize_g(2, 0), lambda: v_g(3, 0, 0, 256)],
-            pe=[lambda: quantize_v(1)],
-            fill=[lambda j=j: moments(0, 512, j, "o%d" % (j % 2)) for j in range(4)],
+            then=[lambda: quantize_g(2, 0), lambda: v_g(3, 0, 0, 256)],
+            scalar=[lambda: quantize_v(1), lambda: out_jobs(0, 4)],
         )
         step(
             7,
-            mid=[lambda: quantize_g(3, 0), lambda: v_g(4, 0, 0, 128), lambda: v_g(4, 1, 0, 128)],
-            fill=[lambda j=j: moments(0, 512, j, "o%d" % (j % 2)) for j in range(4, 8)],
+            then=[lambda: quantize_g(3, 0), lambda: v_g(4, 0, 0, 128), lambda: v_g(4, 1, 0, 128)],
+            scalar=[lambda: out_jobs(4, 8)],
         )
+        v_d(7)
         quantize_g(4, 0)
         quantize_g(4, 1)
-        v_d(7)
-        for j in range(4):
-            moments(512, 256, j, "zm"[j // 2] + str(j % 2))
         v_g(5, 0, 0, 128)
         v_g(5, 1, 0, 128)
-        for j in range(2):
-            moments(768, 128, j, "o%d" % j)
         quantize_g(5, 0)
         quantize_g(5, 1)
-        moments(896, 128, 0, "d0", "s")
-        moments(896, 128, 1, "d1", "v")
+        out_jobs(8, 14)
+
+        q0, wd = UNITS[5][:2]
+        last = [psum.tile([P, BANK], F32, name="last", tag=tag) for tag in ("d0", "d1", "z0", "z1")]
+        for k in range(4):
+            mx(last[k][:, 0:wd], v_op(0, 2 * k), gq_op(0, q0, wd), True, False)
+        for k in range(4):
+            mx(last[k][:, 0:wd], v_op(1, 2 * k), gq_op(1, q0, wd), False, True)
+            for g in range(GROUPS):
+                mx(last[k][:, wd : 2 * wd], v_op(g, 2 * k + 1), gq_op(g, q0, wd), g == 0, g == 1)
+            ot = work.tile([P, BANK], F32, name="ot", bufs=9)
+            scale_out("sv"[k % 2], ot[:, 0 : 2 * wd], last[k][:, 0 : 2 * wd])
+            store(ot, q0, wd, 2 * k, 2)

@@ -178,17 +178,17 @@ def tile_aipwscorebasismoments_d1p_kernel(
         vw = {}
         vi = {}
 
-        def v_widen(g, t):
+        def v_widen(g, t, engine="s"):
             if t == 0:
                 vw[g] = work.tile([P, T, M], BF16, name="vw", bufs=1)
             for j in range(8):
                 cols = slice(j * P, (j + 1) * P)
-                nc.scalar.activation(
-                    out=vw[g][:, t, cols],
-                    in_=vb[g][:, t, cols].bitcast(FP8),
-                    func=ACT.Copy,
-                    scale=vs[:, g, t * 8 + j : t * 8 + j + 1],
-                )
+                dst, src = vw[g][:, t, cols], vb[g][:, t, cols].bitcast(FP8)
+                by = vs[:, g, t * 8 + j : t * 8 + j + 1]
+                if engine == "s":
+                    nc.scalar.activation(out=dst, in_=src, func=ACT.Copy, scale=by)
+                else:
+                    nc.vector.tensor_scalar(out=dst, in0=src, scalar1=by, scalar2=None, op0=ALU.mult)
 
         def v_interleave(g, copy, lo, hi):
             if g not in vi:
@@ -362,9 +362,9 @@ def tile_aipwscorebasismoments_d1p_kernel(
             k3 = kap[u][:, side].rearrange("p (t q) -> p t q", t=T)[:, :, lo:hi]
             d3 = dd[u][:, side].rearrange("p (t q) -> p t q", t=T)[:, :, lo:hi]
             nc.vector.tensor_tensor(
-                out=gi[u][:, i, lo:hi, :].rearrange("p (c i) t -> p c t i", i=4),
-                in0=k3.rearrange("p t (c i) -> p c t i", i=4),
-                in1=d3.rearrange("p t (c i) -> p c t i", i=4),
+                out=gi[u][:, i, lo:hi, :].rearrange("p (c i) t -> p c t i", i=2),
+                in0=k3.rearrange("p t (c i) -> p c t i", i=2),
+                in1=d3.rearrange("p t (c i) -> p c t i", i=2),
                 op=ALU.mult,
             )
 
@@ -419,15 +419,16 @@ def tile_aipwscorebasismoments_d1p_kernel(
         xr[0] = load_x(0)
         nc.sync.dma_start(out=w_sb[:], in_=w_v)
         br[0, 0] = load_b(0, 0)
+        load_gam(0)
         yr[0, 0] = load_y(0, 0)
         load_gam_scales()
-        load_gam(0)
         br[1, 0] = load_b(1, 0)
         lr[0, 0] = load_lat(0, 0)
-        nc.sync.dma_start(out=vs[:], in_=vs_v)
         xr[1] = load_x(1)
         br[0, 1] = load_b(0, 1)
         yr[0, 1] = load_y(0, 1)
+        nc.sync.dma_start(out=vs[:], in_=vs_v)
+        lr[0, 1] = load_lat(0, 1)
         nc.vector.tensor_scalar(
             out=wp[:],
             in0=w_sb[:].rearrange("p g t -> p (g t)"),
@@ -437,45 +438,45 @@ def tile_aipwscorebasismoments_d1p_kernel(
         )
 
         x_transpose(0, ("o0", "o1"))
-        x_copy(0, 0, S)
+        x_copy(0, 0, V)
         x_copy(0, 1, V)
-        quantize_x(0, 0)
-        weigh_y(0, 0, "vv--")
-        b_interleave(0, 0, V, 0, 256)
         b_interleave(0, 0, S, 256, 512)
+        b_interleave(0, 0, V, 0, 256)
+        quantize_x(0, 0)
+        pe_z(0)
         negate_x(0, "v")
         quantize_b(0, 0)
+        weigh_y(0, 0, "svss")
         quantize_x(0, 1)
-        pe_z(0)
-        pe_mu0(0)
         b_interleave(1, 0, G, 0, 256)
+        pe_mu0(0)
         s_exp(0)
-        b_interleave(1, 0, S, 256, 512)
-        weigh_y(0, 0, "--ss")
         pe_z(1)
         s_exp(1)
+        b_interleave(1, 0, V, 256, 512)
         v_h(0)
-        treat(0, 0)
         clip(0, nc.vector)
-        quantize_b(1, 0)
         pe_mu0(1)
+        quantize_b(1, 0)
+        treat(0, 0)
         v_f(0)
         clip(1)
         v_kap(0)
+        b_interleave(0, 1, S, 0, 512)
         x_transpose(1, ("o0", "o1"))
         pe_d(0)
         x_copy(1, 0, S)
         x_copy(1, 1, S)
-        weigh_y(0, 1, "ssss")
+        weigh_y(0, 1, "ss-s")
         br[1, 1] = load_b(1, 1)
         load_gam(1)
-        lr[0, 1] = load_lat(0, 1)
         yr[1, 0] = load_y(1, 0)
         vb[0] = load_v(0)
         lr[1, 0] = load_lat(1, 0)
         vb[1] = load_v(1)
+        weigh_y(0, 1, "--g-")
 
-        def step(n, late_z=False, then=(), end=(), scalar=()):
+        def step(n, late_z=False, then=(), end=(), after=()):
             if n + 1 < n_steps and not late_z:
                 pe_z(n + 1)
                 s_exp(n + 1)
@@ -496,61 +497,76 @@ def tile_aipwscorebasismoments_d1p_kernel(
             for f in end:
                 f()
             v_kap(n)
-            for f in scalar:
+            for f in after:
                 f()
 
         def late_loads():
             yr[1, 1] = load_y(1, 1)
             lr[1, 1] = load_lat(1, 1)
 
-        def out_jobs(lo, hi, engine="s"):
+        def out_jobs(lo, hi):
             banks_free = ("o0", "o1", "z0", "z1", "m0", "m1")
             jobs = [(0, 512, j) for j in range(8)] + [(512, 256, j) for j in range(4)] + [(768, 128, j) for j in range(2)]
             for i in range(lo, hi):
-                moments(*jobs[i], banks_free[i % 6], engine)
+                moments(*jobs[i], banks_free[i % 6], "s")
 
-        b_interleave(0, 1, S, 0, 512)
         step(
             1,
             late_z=True,
-            then=[lambda: quantize_x(1, 0), lambda: negate_x(1, "v"), lambda: treat(0, 1)],
-            end=[lambda: quantize_x(1, 1)],
-            scalar=[lambda: b_interleave(1, 1, G, 0, 128), lambda: b_interleave(1, 1, S, 128, 512), late_loads],
+            then=[
+                lambda: quantize_x(1, 0),
+                lambda: negate_x(1, "v"),
+                lambda: treat(0, 1),
+                lambda: quantize_x(1, 1),
+            ],
+            end=[lambda: quantize_b(0, 1)],
+            after=[lambda: b_interleave(1, 1, G, 0, 128), lambda: b_interleave(1, 1, S, 128, 512)],
         )
         step(
             2,
-            then=[lambda: v_g(0, 0, 0, 256), lambda: v_g(0, 0, 256, 512)],
-            end=[lambda: quantize_b(0, 1)],
-            scalar=[lambda: weigh_y(1, 0, "ssss")] + [lambda t=t: v_widen(0, t) for t in range(4)],
+            after=[
+                late_loads,
+                lambda: v_g(0, 0, 0, 256),
+                lambda: v_g(0, 0, 256, 512),
+                lambda: weigh_y(1, 0, "ssgs"),
+            ]
+            + [lambda t=t: v_widen(0, t) for t in range(4)],
         )
         step(
             3,
             then=[lambda: quantize_b(1, 1), lambda: quantize_g(0, 0)],
-            scalar=[lambda: treat(1, 0), lambda: weigh_y(1, 1, "ssss"), lambda: v_interleave(0, G, 0, 128), lambda: v_interleave(0, S, 128, 512)],
+            after=[lambda: weigh_y(1, 1, "ssss"), lambda: v_interleave(0, S, 0, 512)],
         )
         step(
             4,
-            then=[lambda: v_g(1, 0, 0, 256), lambda: v_g(1, 0, 256, 512)],
-            scalar=[lambda: v_interleave(0, G, 512, 640), lambda: v_interleave(0, S, 640, 1024)] + [lambda t=t: v_widen(1, t) for t in range(3)],
+            then=[lambda: v_g(1, 0, 0, 256), lambda: treat(1, 0), lambda: treat(1, 1)],
+            end=[lambda: v_g(1, 0, 256, 512)],
+            after=[lambda: v_interleave(0, G, 512, 640), lambda: v_interleave(0, S, 640, 1024)],
         )
         step(
             5,
-            then=[lambda: quantize_g(1, 0), lambda: v_g(2, 0, 0, 256), lambda: quantize_v(0), lambda: treat(1, 1)],
-            scalar=[lambda: v_widen(1, 3), lambda: v_interleave(1, G, 0, 128), lambda: v_interleave(1, S, 128, 512), lambda: v_interleave(1, S, 512, 1024)],
+            then=[lambda: quantize_g(1, 0), lambda: quantize_v(0), lambda: v_widen(1, 0, "v")],
+            end=[lambda: v_g(2, 0, 0, 256)],
+            after=[lambda t=t: v_widen(1, t) for t in range(1, 4)]
+            + [
+                lambda: v_interleave(1, G, 0, 128),
+                lambda: v_interleave(1, S, 128, 512),
+                lambda: v_interleave(1, S, 512, 1024),
+            ],
         )
         step(
             6,
             then=[lambda: quantize_g(2, 0), lambda: v_g(3, 0, 0, 256)],
-            scalar=[lambda: quantize_v(1), lambda: out_jobs(0, 4)],
+            end=[lambda: quantize_v(1)],
+            after=[lambda: out_jobs(0, 4)],
         )
         step(
             7,
             then=[lambda: quantize_g(3, 0), lambda: v_g(4, 0, 0, 128), lambda: v_g(4, 1, 0, 128)],
-            scalar=[lambda: out_jobs(4, 8)],
+            end=[lambda: quantize_g(4, 0), lambda: quantize_g(4, 1)],
+            after=[lambda: out_jobs(4, 8)],
         )
         v_d(7)
-        quantize_g(4, 0)
-        quantize_g(4, 1)
         v_g(5, 0, 0, 128)
         v_g(5, 1, 0, 128)
         quantize_g(5, 0)

import math
from contextlib import ExitStack

import concourse.mybir as mybir
from concourse.masks import make_identity

N, K, Q, M = 1024, 512, 1024, 1024
FLOPS = 2 * (3 * N * K * Q + N * M * Q)

F32 = mybir.dt.float32
BF16 = mybir.dt.bfloat16
I32 = mybir.dt.int32
U32 = mybir.dt.uint32
U8 = mybir.dt.uint8
FP8 = mybir.dt.float8_e4m3fn
FP8X4 = mybir.dt.float8_e4m3fn_x4
ALU = mybir.AluOpType
ACT = mybir.ActivationFunctionType

P = 128
T = 4
GROUPS = 2
HALF = 512
BANK = 512
PMIN, PMAX = 0.15, 0.85
ODDS_LO, ODDS_HI = 3.0 / 17.0, 17.0 / 3.0
UNITS = (
    (0, 512, (0,)),
    (0, 512, (1,)),
    (512, 256, (0,)),
    (512, 256, (1,)),
    (768, 128, (0, 1)),
    (896, 128, (0, 1)),
)
STEP_COLS = 2 * BANK


def tile_aipwscorebasismoments_d1p_kernel(
    tc, x, b, gam_words, gam_scales, lat, y, v_bytes, v_scale, w, out
):
    nc = tc.nc
    x_v = x.rearrange("(g m t) k -> m g t k", g=GROUPS, t=T)
    b_v = b.rearrange("a (p j) q -> p a j q", j=T)
    lat_v = lat.rearrange("(g p t) q -> p g t q", g=GROUPS, t=T)
    y_v = y.rearrange("(g p t) q -> p g t q", g=GROUPS, t=T)
    v_v = v_bytes.rearrange("(g p t) m -> p g t m", g=GROUPS, t=T)
    vs_v = v_scale.rearrange("(g p t) j -> p g (t j)", g=GROUPS, t=T)
    w_v = w.rearrange("(g p t) -> p g t", g=GROUPS, t=T)
    gam_v = gam_words[0].rearrange("p n t -> p (n t)")

    steps = []
    for u, (q0, wd, groups) in enumerate(UNITS):
        slices = [(g, t) for g in groups for t in range(T)]
        per = STEP_COLS // wd
        steps += [(u, k, slices[k : k + per]) for k in range(0, len(slices), per)]
    n_steps = len(steps)

    with ExitStack() as ctx:
        keep = ctx.enter_context(tc.tile_pool(name="keep", bufs=1))
        work = ctx.enter_context(tc.tile_pool(name="work", bufs=2))
        psum = ctx.enter_context(tc.psum_pool(name="psum", bufs=1))
        ctx.enter_context(tc.manual_schedule())

        ident = keep.tile([P, P], F32, name="ident")
        xq = keep.tile([P, 2, GROUPS * T, P], U32, name="xq", align_bytes=64)
        xqs = keep.tile([P, 2, GROUPS * T, P], U8, name="xqs", align_bytes=64)
        bq = keep.tile([P, 2, Q], U32, name="bq", align_bytes=64)
        bqs = keep.tile([P, 2, Q], U8, name="bqs", align_bytes=64)
        gw = keep.tile([P, Q * T], U8, name="gw", align_bytes=64)
        gs = keep.tile([P, Q], U8, name="gs", align_bytes=64)
        vq = keep.tile([P, GROUPS, M], U32, name="vq", align_bytes=64)
        vqs = keep.tile([P, GROUPS, M], U8, name="vqs", align_bytes=64)
        gq = keep.tile([P, GROUPS, Q], U32, name="gq", align_bytes=64)
        gqs = keep.tile([P, GROUPS, Q], U8, name="gqs", align_bytes=64)
        w_sb = keep.tile([P, GROUPS, T], BF16, name="w_sb")
        wp = keep.tile([P, GROUPS * T], F32, name="wp")
        vs = keep.tile([P, GROUPS, T * 8], F32, name="vs")
        zero = keep.tile([P, 1], F32, name="zero")
        bias = keep.tile([P, 1], F32, name="bias")
        warm = keep.tile([P, 1], F32, name="warm")

        def load_x(g):
            xr = work.tile([P, T, K], BF16, name="xr", tag="s4", align_bytes=64)
            nc.sync.dma_start(out=xr[:], in_=x_v[:, g])
            return xr

        def load_b(a, h):
            br = work.tile([P, T, HALF], BF16, name="br", bufs=3)
            nc.sync.dma_start(out=br[:], in_=b_v[:, a, :, h * HALF : (h + 1) * HALF])
            return br

        def load_gam(h):
            cols = slice(h * HALF * T, (h + 1) * HALF * T)
            nc.sync.dma_start(out=gw[:, cols].bitcast(I32), in_=gam_v[:, cols].bitcast(I32))

        def load_gam_scales():
            for quad in range(4):
                nc.sync.dma_start(
                    out=gs[32 * quad : 32 * quad + 4, :].bitcast(I32),
                    in_=gam_scales[0, 4 * quad : 4 * quad + 4, :].bitcast(I32),
                )

        def load_y(h, g):
            yr = work.tile([P, T, HALF], BF16, name="yr")
            nc.sync.dma_start(out=yr[:], in_=y_v[:, g, :, h * HALF : (h + 1) * HALF])
            return yr

        def load_lat(h, g):
            lr = work.tile([P, T, HALF], BF16, name="lr")
            nc.sync.dma_start(out=lr[:], in_=lat_v[:, g, :, h * HALF : (h + 1) * HALF])
            return lr

        def load_v(g):
            vb = work.tile([P, T, M], U8, name="vb")
            nc.sync.dma_start(out=vb[:], in_=v_v[:, g])
            return vb

        xg = {}
        xps = {}
        xn = {}

        def x_transpose(g, tags):
            words = xr[g][:].bitcast(F32)
            xps[g] = []
            for half in range(2):
                xp = psum.tile([P, 2, 2, P], F32, name="xp", tag=tags[half])
                for i in range(2):
                    for u in range(2):
                        nc.tensor.transpose(xp[:, i, u, :], words[:, 2 * half + i, u : K // 2 : 2], ident[:])
                xps[g].append(xp)
            xg[g] = work.tile([P, T, P, T], BF16, name="xg", tag="s4b", bufs=3, align_bytes=64)

        def x_copy(g, half, copy):
            copy(
                out=xg[g][:, 2 * half : 2 * half + 2].bitcast(F32),
                in_=xps[g][half][:].rearrange("p s u r -> p s r u"),
            )

        def quantize_x(g, sign):
            words = slice(g * T, (g + 1) * T)
            src = xg[g][:].rearrange("p s r t -> p (s r t)") if sign == 0 else xn[g][:]
            nc.vector.quantize_mx(
                out=xq[:, sign, words, :].rearrange("p s r -> p (s r)").bitcast(FP8X4),
                scales=xqs[:, sign, words, :].rearrange("p s r -> p (s r)"),
                in_=src,
            )

        def negate_x(g, engine):
            xn[g] = work.tile([P, T * P * T], BF16, name="xn", bufs=1, align_bytes=64)
            src = xg[g][:].rearrange("p s r t -> p (s r t)")
            if engine == "s":
                nc.scalar.activation(out=xn[g][:], in_=src, func=ACT.Copy, scale=-1.0)
            else:
                nc.vector.tensor_scalar(out=xn[g][:], in0=src, scalar1=-1.0, scalar2=None, op0=ALU.mult)

        def interleave(copy, dst, src):
            if copy is G:
                copy(out=dst, in_=src.rearrange("p t q -> p q t"))
                return
            copy(
                out=dst.rearrange("p (c i) t -> p c t i", i=4),
                in_=src.rearrange("p t (c i) -> p c t i", i=4),
            )

        bi = {}

        def b_interleave(a, h, copy, lo, hi):
            if (a, h) not in bi:
                bi[a, h] = work.tile([P, HALF, T], BF16, name="bi", align_bytes=64)
            interleave(copy, bi[a, h][:, lo:hi, :], br[a, h][:, :, lo:hi])

        def quantize_b(a, h):
            cols = slice(h * HALF, (h + 1) * HALF)
            nc.vector.quantize_mx(
                out=bq[:, a, cols].bitcast(FP8X4), scales=bqs[:, a, cols], in_=bi[a, h][:].rearrange("p q t -> p (q t)")
            )

        vw = {}
        vi = {}

        def v_widen(g, t, engine="s"):
            if t == 0:
                vw[g] = work.tile([P, T, M], BF16, name="vw", bufs=1)
            for j in range(8):
                cols = slice(j * P, (j + 1) * P)
                dst, src = vw[g][:, t, cols], vb[g][:, t, cols].bitcast(FP8)
                by = vs[:, g, t * 8 + j : t * 8 + j + 1]
                if engine == "s":
                    nc.scalar.activation(out=dst, in_=src, func=ACT.Copy, scale=by)
                else:
                    nc.vector.tensor_scalar(out=dst, in0=src, scalar1=by, scalar2=None, op0=ALU.mult)

        def v_interleave(g, copy, lo, hi):
            if g not in vi:
                vi[g] = work.tile([P, M, T], BF16, name="vi", bufs=1, align_bytes=64)
            interleave(copy, vi[g][:, lo:hi, :], vw[g][:, :, lo:hi])

        def quantize_v(g):
            nc.vector.quantize_mx(
                out=vq[:, g, :].bitcast(FP8X4), scales=vqs[:, g, :], in_=vi[g][:].rearrange("p m t -> p (m t)")
            )

        yw = {}
        tb = {}

        def weigh_y(h, g, engines):
            if (h, g) not in yw:
                yw[h, g] = work.tile([P, T, HALF], F32, name="yw")
            for t in range(T):
                if engines[t] == "-":
                    continue
                dst, src, by = yw[h, g][:, t, :], yr[h, g][:, t, :], wp[:, g * T + t : g * T + t + 1]
                if engines[t] == "s":
                    nc.scalar.activation(out=dst, in_=src, func=ACT.Copy, scale=by)
                else:
                    engine = nc.vector if engines[t] == "v" else nc.gpsimd
                    engine.tensor_scalar(out=dst, in0=src, scalar1=by, scalar2=1.0, op0=ALU.mult, op1=ALU.mult)

        def treat(h, g):
            tb[h, g] = work.tile([P, T, HALF], F32, name="tb")
            nc.vector.tensor_scalar(
                out=tb[h, g][:], in0=lr[h, g][:], scalar1=0.0, scalar2=PMIN, op0=ALU.is_gt, op1=ALU.subtract
            )

        def mx(o, lhs, rhs, start, stop):
            nc.tensor.matmul_mx(
                out=o, lhsT=lhs[0], lhsT_scale=lhs[1], rhs=rhs[0], rhs_scale=rhs[1], start=start, stop=stop
            )

        def x_op(sign, g, t):
            return xq[:, sign, g * T + t, :].bitcast(FP8X4), xqs[:, sign, g * T + t, :]

        def b_op(a, q0, wd):
            return bq[:, a, q0 : q0 + wd].bitcast(FP8X4), bqs[:, a, q0 : q0 + wd]

        def gam_op(q0, wd):
            return gw[:, q0 * T : (q0 + wd) * T].bitcast(FP8X4), gs[:, q0 : q0 + wd]

        banks = {}

        def places(n):
            u, k0, slices = steps[n]
            wd = UNITS[u][1]
            return [(g, t, i * wd // BANK, i * wd % BANK) for i, (g, t) in enumerate(slices)]

        def new_banks(kind, n):
            banks[kind, n] = [psum.tile([P, BANK], F32, name=kind, tag="%s%d" % (kind, j)) for j in range(2)]
            return banks[kind, n]

        def pe_z(n):
            q0, wd = UNITS[steps[n][0]][:2]
            o = new_banks("z", n)
            for g, t, j, col in places(n):
                mx(o[j][:, col : col + wd], x_op(0, g, t), gam_op(q0, wd), True, True)

        def pe_mu0(n):
            q0, wd = UNITS[steps[n][0]][:2]
            o = new_banks("m", n)
            for g, t, j, col in places(n):
                mx(o[j][:, col : col + wd], x_op(0, g, t), b_op(0, q0, wd), True, True)

        def pe_d(n):
            q0, wd = UNITS[steps[n][0]][:2]
            o = new_banks("d", n)
            for g, t, j, col in places(n):
                mx(o[j][:, col : col + wd], x_op(0, g, t), b_op(1, q0, wd), True, False)
                mx(o[j][:, col : col + wd], x_op(1, g, t), b_op(0, q0, wd), False, True)

        raw = {}
        odds = {}
        kap = {}
        res = {}
        dd = {}
        gi = {}

        def unit_tile(store, u, name, bufs):
            q0, wd, groups = UNITS[u]
            if u not in store:
                size = len(groups) * T * wd
                tag, n_bufs = bufs[size]
                store[u] = work.tile([P, size], F32, name=name, tag=tag, bufs=n_bufs, align_bytes=64)
            return store[u]

        def s_exp(n):
            u, k0, slices = steps[n]
            base = k0 * UNITS[u][1]
            k = unit_tile(kap, u, "kap", {2048: ("kap", 2), 1024: ("s4b", 3)})
            raw[n] = work.tile([P, STEP_COLS], F32, name="raw")
            for j in range(2):
                nc.scalar.activation(
                    out=k[:, base + j * BANK : base + (j + 1) * BANK],
                    in_=banks["z", n][j][:],
                    func=ACT.Exp,
                    scale=-1.0,
                    bias=bias[:],
                )
                nc.scalar.activation(out=raw[n][:, j * BANK : (j + 1) * BANK], in_=banks["z", n][j][:], func=ACT.Exp)

        def clip(n, engine=nc.gpsimd):
            odds[n] = work.tile([P, STEP_COLS], F32, name="odds", bufs=1)
            engine.tensor_scalar(
                out=odds[n][:], in0=raw[n][:], scalar1=ODDS_HI, scalar2=ODDS_LO, op0=ALU.min, op1=ALU.max
            )

        def v_h(n):
            q0, wd = UNITS[steps[n][0]][:2]
            off = q0 % HALF
            res[n] = work.tile([P, STEP_COLS], F32, name="res")
            for g, t, j, col in places(n):
                nc.vector.scalar_tensor_tensor(
                    out=res[n][:, j * BANK + col : j * BANK + col + wd],
                    in0=banks["m", n][j][:, col : col + wd],
                    scalar=wp[:, g * T + t : g * T + t + 1],
                    in1=yw[q0 // HALF, g][:, t, off : off + wd],
                    op0=ALU.mult,
                    op1=ALU.subtract,
                )

        def v_kap(n):
            u, k0, slices = steps[n]
            q0, wd, groups = UNITS[u]
            off = q0 % HALF
            for i in range(0, len(slices), T):
                part = slices[i : i + T]
                g, t0 = part[0]
                lo, hi = (k0 + i) * wd, (k0 + i + len(part)) * wd
                k3 = kap[u][:, lo:hi].rearrange("p (t q) -> p t q", q=wd)
                nc.vector.scalar_tensor_tensor(
                    out=k3,
                    in0=k3,
                    scalar=PMIN * ODDS_LO,
                    in1=tb[q0 // HALF, g][:, t0 : t0 + len(part), off : off + wd],
                    op0=ALU.max,
                    op1=ALU.min,
                )

        def v_f(n):
            nc.vector.scalar_tensor_tensor(
                out=res[n][:], in0=odds[n][:], scalar=1.0, in1=res[n][:], op0=ALU.add, op1=ALU.mult
            )

        def v_d(n, part=slice(None)):
            u, k0, slices = steps[n]
            q0, wd = UNITS[u][:2]
            d = unit_tile(dd, u, "dd", {2048: ("dd", 2), 1024: ("dd", 2)})
            for i, (g, t, j, col) in list(enumerate(places(n)))[part]:
                lo = (k0 + i) * wd
                nc.vector.scalar_tensor_tensor(
                    out=d[:, lo : lo + wd],
                    in0=banks["d", n][j][:, col : col + wd],
                    scalar=wp[:, g * T + t : g * T + t + 1],
                    in1=res[n][:, j * BANK + col : j * BANK + col + wd],
                    op0=ALU.mult,
                    op1=ALU.add,
                )

        def v_g(u, i, lo, hi):
            q0, wd, groups = UNITS[u]
            if u not in gi:
                gi[u] = work.tile([P, len(groups), wd, T], BF16, name="gi", tag="s4", align_bytes=64)
            side = slice(i * T * wd, (i + 1) * T * wd)
            k3 = kap[u][:, side].rearrange("p (t q) -> p t q", t=T)[:, :, lo:hi]
            d3 = dd[u][:, side].rearrange("p (t q) -> p t q", t=T)[:, :, lo:hi]
            nc.vector.tensor_tensor(
                out=gi[u][:, i, lo:hi, :].rearrange("p (c i) t -> p c t i", i=2),
                in0=k3.rearrange("p t (c i) -> p c t i", i=2),
                in1=d3.rearrange("p t (c i) -> p c t i", i=2),
                op=ALU.mult,
            )

        def quantize_g(u, i):
            q0, wd, groups = UNITS[u]
            nc.vector.quantize_mx(
                out=gq[:, groups[i], q0 : q0 + wd].bitcast(FP8X4),
                scales=gqs[:, groups[i], q0 : q0 + wd],
                in_=gi[u][:, i].rearrange("p q t -> p (q t)"),
            )

        def v_op(g, m):
            return vq[:, g, m * P : (m + 1) * P].bitcast(FP8X4), vqs[:, g, m * P : (m + 1) * P]

        def gq_op(g, q0, wd):
            return gq[:, g, q0 : q0 + wd].bitcast(FP8X4), gqs[:, g, q0 : q0 + wd]

        def scale_out(engine, dst, src):
            if engine == "s":
                nc.scalar.activation(out=dst, in_=src, func=ACT.Copy, scale=1.0 / 32.0)
            else:
                nc.vector.tensor_scalar(out=dst, in0=src, scalar1=1.0 / 32.0, scalar2=None, op0=ALU.mult)

        def store(ot, q0, wd, m0, tiles):
            nc.sync.dma_start(
                out=out[m0 * P : (m0 + tiles) * P, q0 : q0 + wd].rearrange("(i m) q -> m i q", i=tiles),
                in_=ot[:, 0 : tiles * wd].rearrange("m (i q) -> m i q", i=tiles),
            )

        def moments(q0, wd, job, tag, engine):
            per = BANK // wd
            o = psum.tile([P, BANK], F32, name="o", tag=tag)
            for i in range(per):
                for g in range(GROUPS):
                    mx(o[:, i * wd : (i + 1) * wd], v_op(g, job * per + i), gq_op(g, q0, wd), g == 0, g == 1)
            ot = work.tile([P, BANK], F32, name="ot", bufs=9)
            scale_out(engine, ot[:], o[:])
            store(ot, q0, wd, job * per, per)

        S, V = nc.scalar.copy, nc.vector.tensor_copy

        def G(out, in_):
            nc.gpsimd.tensor_scalar(out=out, in0=in_, scalar1=1.0, scalar2=0.0, op0=ALU.mult, op1=ALU.add)

        nc.vector.memset(gs[:].bitcast(I32), 0)
        nc.vector.memset(zero[:], 0.0)
        nc.vector.tensor_scalar(out=bias[:], in0=zero[:], scalar1=math.log(PMIN), scalar2=None, op0=ALU.add)
        nc.scalar.activation(out=warm[:], in_=zero[:], func=ACT.Exp)
        make_identity(nc, ident[:])

        xr, br, yr, lr, vb = {}, {}, {}, {}, {}
        xr[0] = load_x(0)
        nc.sync.dma_start(out=w_sb[:], in_=w_v)
        br[0, 0] = load_b(0, 0)
        load_gam(0)
        yr[0, 0] = load_y(0, 0)
        load_gam_scales()
        br[1, 0] = load_b(1, 0)
        lr[0, 0] = load_lat(0, 0)
        xr[1] = load_x(1)
        br[0, 1] = load_b(0, 1)
        yr[0, 1] = load_y(0, 1)
        nc.sync.dma_start(out=vs[:], in_=vs_v)
        lr[0, 1] = load_lat(0, 1)
        nc.vector.tensor_scalar(
            out=wp[:],
            in0=w_sb[:].rearrange("p g t -> p (g t)"),
            scalar1=-1.0 / PMIN,
            scalar2=None,
            op0=ALU.mult,
        )

        x_transpose(0, ("o0", "o1"))
        x_copy(0, 0, V)
        x_copy(0, 1, V)
        b_interleave(0, 0, S, 256, 512)
        b_interleave(0, 0, V, 0, 256)
        quantize_x(0, 0)
        pe_z(0)
        negate_x(0, "v")
        quantize_b(0, 0)
        weigh_y(0, 0, "svss")
        quantize_x(0, 1)
        b_interleave(1, 0, G, 0, 256)
        pe_mu0(0)
        s_exp(0)
        pe_z(1)
        s_exp(1)
        b_interleave(1, 0, V, 256, 512)
        v_h(0)
        clip(0, nc.vector)
        pe_mu0(1)
        quantize_b(1, 0)
        treat(0, 0)
        v_f(0)
        clip(1)
        v_kap(0)
        b_interleave(0, 1, S, 0, 512)
        x_transpose(1, ("o0", "o1"))
        pe_d(0)
        x_copy(1, 0, S)
        x_copy(1, 1, S)
        weigh_y(0, 1, "ss-s")
        br[1, 1] = load_b(1, 1)
        load_gam(1)
        yr[1, 0] = load_y(1, 0)
        vb[0] = load_v(0)
        lr[1, 0] = load_lat(1, 0)
        vb[1] = load_v(1)
        weigh_y(0, 1, "--g-")

        def step(n, late_z=False, then=(), end=(), after=()):
            if n + 1 < n_steps and not late_z:
                pe_z(n + 1)
                s_exp(n + 1)
            v_d(n - 1)
            v_h(n)
            pe_d(n)
            if n + 1 < n_steps and not late_z:
                pe_mu0(n + 1)
            for f in then:
                f()
            if late_z:
                pe_z(n + 1)
                s_exp(n + 1)
                pe_mu0(n + 1)
            v_f(n)
            if n + 1 < n_steps:
                clip(n + 1)
            for f in end:
                f()
            v_kap(n)
            for f in after:
                f()

        def late_loads():
            yr[1, 1] = load_y(1, 1)
            lr[1, 1] = load_lat(1, 1)

        def out_jobs(lo, hi):
            banks_free = ("o0", "o1", "z0", "z1", "m0", "m1")
            jobs = [(0, 512, j) for j in range(8)] + [(512, 256, j) for j in range(4)] + [(768, 128, j) for j in range(2)]
            for i in range(lo, hi):
                moments(*jobs[i], banks_free[i % 6], "s")

        step(
            1,
            late_z=True,
            then=[
                lambda: quantize_x(1, 0),
                lambda: negate_x(1, "v"),
                lambda: treat(0, 1),
                lambda: quantize_x(1, 1),
            ],
            end=[lambda: quantize_b(0, 1)],
            after=[lambda: b_interleave(1, 1, G, 0, 128), lambda: b_interleave(1, 1, S, 128, 512)],
        )
        step(
            2,
            after=[
                late_loads,
                lambda: v_g(0, 0, 0, 256),
                lambda: v_g(0, 0, 256, 512),
                lambda: weigh_y(1, 0, "ssgs"),
            ]
            + [lambda t=t: v_widen(0, t) for t in range(4)],
        )
        step(
            3,
            then=[lambda: quantize_b(1, 1), lambda: quantize_g(0, 0)],
            after=[lambda: weigh_y(1, 1, "ssss"), lambda: v_interleave(0, S, 0, 512)],
        )
        step(
            4,
            then=[lambda: v_g(1, 0, 0, 256), lambda: treat(1, 0), lambda: treat(1, 1)],
            end=[lambda: v_g(1, 0, 256, 512)],
            after=[lambda: v_interleave(0, G, 512, 640), lambda: v_interleave(0, S, 640, 1024)],
        )
        step(
            5,
            then=[lambda: quantize_g(1, 0), lambda: quantize_v(0), lambda: v_widen(1, 0, "v")],
            end=[lambda: v_g(2, 0, 0, 256)],
            after=[lambda t=t: v_widen(1, t) for t in range(1, 4)]
            + [
                lambda: v_interleave(1, G, 0, 128),
                lambda: v_interleave(1, S, 128, 512),
                lambda: v_interleave(1, S, 512, 1024),
            ],
        )
        step(
            6,
            then=[lambda: quantize_g(2, 0), lambda: v_g(3, 0, 0, 256)],
            end=[lambda: quantize_v(1)],
            after=[lambda: out_jobs(0, 4)],
        )
        step(
            7,
            then=[lambda: quantize_g(3, 0), lambda: v_g(4, 0, 0, 128), lambda: v_g(4, 1, 0, 128)],
            end=[lambda: quantize_g(4, 0), lambda: quantize_g(4, 1)],
            after=[lambda: out_jobs(4, 8)],
        )
        v_d(7)
        v_g(5, 0, 0, 128)
        v_g(5, 1, 0, 128)
        quantize_g(5, 0)
        quantize_g(5, 1)
        out_jobs(8, 14)

        q0, wd = UNITS[5][:2]
        last = [psum.tile([P, BANK], F32, name="last", tag=tag) for tag in ("d0", "d1", "z0", "z1")]
        for k in range(4):
            mx(last[k][:, 0:wd], v_op(0, 2 * k), gq_op(0, q0, wd), True, False)
        for k in range(4):
            mx(last[k][:, 0:wd], v_op(1, 2 * k), gq_op(1, q0, wd), False, True)
            for g in range(GROUPS):
                mx(last[k][:, wd : 2 * wd], v_op(g, 2 * k + 1), gq_op(g, q0, wd), g == 0, g == 1)
            ot = work.tile([P, BANK], F32, name="ot", bufs=9)
            scale_out("sv"[k % 2], ot[:, 0 : 2 * wd], last[k][:, 0 : 2 * wd])
            store(ot, q0, wd, 2 * k, 2)
